import numpy as np
import ml_dtypes


def mxq(x, axis, fmt="e4m3"):
    dtype, down = {"e4m3": (ml_dtypes.float8_e4m3fn, 7), "e5m2": (ml_dtypes.float8_e5m2, 14)}[fmt]
    v = np.moveaxis(np.asarray(x, np.float32).astype(ml_dtypes.bfloat16).astype(np.float64), axis, -1)
    blocks = v.reshape(v.shape[:-1] + (-1, 32))
    amax = np.abs(blocks).max(-1, keepdims=True)
    byte = np.maximum(np.where(amax > 0, np.frexp(amax)[1] - 1 + 127, 0) - down, 1)
    scale = np.exp2(byte - 127.0)
    codes = (blocks / scale).astype(np.float32).astype(dtype).astype(np.float64)
    return np.moveaxis((codes * scale).reshape(v.shape), -1, axis)


WIDE = False


def mx_kscale(k):
    if not WIDE:
        return np.ones(k)
    levels = np.array([10, -10, 5, -5, 0])
    if k % 512:
        return np.exp2(np.random.permutation(np.resize(levels, k // 32))).repeat(32)
    a = np.empty((k // 512, 16))
    for p in range(k // 512):
        a[p, :8] = np.random.permutation(np.resize(levels, 8))
        for g in range(8):
            far = levels[np.abs(levels - a[p, g]) >= 10]
            a[p, g + 8] = far[np.random.randint(len(far))]
    return np.exp2(a.ravel()).repeat(32)


def f64(x):
    return np.asarray(x).astype(np.float64)


def striped(idx):
    return np.tile(idx.reshape(-1, 16).T, (8, 1)).astype(np.uint16)


def unstriped(offs):
    return offs[:16].T.reshape(-1).astype(np.int64)


def pack_weight(w):
    k, n = w.shape
    w = f64(np.asarray(w, np.float32).astype(ml_dtypes.bfloat16)).reshape(k // 32, 32, n)
    amax = np.abs(w).max(1)
    byte = np.clip(np.where(amax > 0, np.frexp(amax)[1] - 1 + 127 - 7, 1), 1, 254)
    scaled = (w * np.exp2(127.0 - byte)[:, None, :]).reshape(k, n).astype(np.float32)
    words = np.ascontiguousarray(scaled.reshape(k // 512, 128, 4, n).transpose(0, 1, 3, 2)).astype(ml_dtypes.float8_e4m3fn).view(np.uint8)
    return words, np.ascontiguousarray(byte.astype(np.uint8).reshape(k // 512, 16, n))


def unpack_weight(words, scales):
    g, p, n, _ = words.shape
    vals = np.ascontiguousarray(words).view(ml_dtypes.float8_e4m3fn).astype(np.float64) * np.repeat(np.exp2(scales.astype(np.float64) - 127.0), 8, axis=1)[..., None]
    return vals.transpose(0, 1, 3, 2).reshape(g * 512, n)


E2M1 = np.array([0.0, 0.5, 1.0, 1.5, 2.0, 3.0, 4.0, 6.0, -0.0, -0.5, -1.0, -1.5, -2.0, -3.0, -4.0, -6.0])


def pack_fp4(w):
    k, n = w.shape
    w = f64(np.asarray(w, np.float32).astype(ml_dtypes.bfloat16)).reshape(k // 32, 32, n)
    amax = np.abs(w).max(1)
    mant, ex = np.frexp(amax / 6.0)
    byte = np.clip(np.where(amax > 0, np.where(mant > 0.5, ex, ex - 1) + 127, 1), 1, 254)
    scaled = (w * np.exp2(127.0 - byte)[:, None, :]).reshape(k, n).astype(np.float32)
    c = np.ascontiguousarray(scaled.reshape(k // 512, 128, 4, n).transpose(0, 1, 3, 2)).astype(ml_dtypes.float4_e2m1fn).view(np.uint8) & 0xF
    words = (c[..., 0::2] | (c[..., 1::2] << 4)).reshape(k // 512, 128, 2 * n)
    return np.ascontiguousarray(words), np.ascontiguousarray(byte.astype(np.uint8).reshape(k // 512, 16, n))


def unpack_fp4(words, scales):
    g, _, n = scales.shape
    words = np.ascontiguousarray(words).reshape(g, 128, n, 2)
    nib = np.empty((g, 128, n, 4), np.uint8)
    nib[..., 0::2] = words & 0xF
    nib[..., 1::2] = words >> 4
    vals = E2M1[nib] * np.repeat(np.exp2(scales.astype(np.float64) - 127.0), 8, axis=1)[..., None]
    return vals.transpose(0, 1, 3, 2).reshape(g * 512, n)


def relu(v):
    return np.maximum(v, 0.0)


K, T, S, D, N, H, V, U = 512, 4096, 1024, 4, 128, 512, 256, 512


def setup_inputs():
    n = np.random.standard_normal
    s = mx_kscale(K)[:, None]
    u = mx_kscale(H)
    packed_xT = pack_weight(n((K, T)) * s)
    packed_w1 = pack_fp4(n((K, H)) / np.sqrt(K) / s)
    packed_w2 = pack_fp4(n((H, N)) / np.sqrt(H) / u[:, None])
    return {
        "x_words": packed_xT[0],
        "x_scales": packed_xT[1],
        "w1_words": packed_w1[0],
        "w1_scales": packed_w1[1],
        "rec": (np.random.uniform(-0.6, 1.2, (H, U))).astype(np.float32),
        "unit": (np.random.uniform(0.6, 1.4, (H, 1)) * u[:, None]).astype(np.float32),
        "w2_words": packed_w2[0],
        "w2_scales": packed_w2[1],
        "offs": striped(np.random.permutation(T)[:S]),
        "pix": striped(np.random.permutation(np.concatenate([np.arange(V), np.random.randint(0, V, U - V)]))),
    }


def reference(x_words, x_scales, w1_words, w1_scales, rec, unit, w2_words, w2_scales, offs, pix):
    xq = unpack_weight(x_words, x_scales)[:, unstriped(offs)]
    y = unpack_fp4(w1_words, w1_scales).T @ xq
    dep = np.tanh(y)
    d2 = (dep) ** 2
    mom2 = d2.reshape(len(d2), -1, D).mean(axis=2)
    ma = mom2[:, unstriped(pix)]
    mom1 = dep.reshape(len(dep), -1, D).mean(axis=2)
    mb = mom1[:, unstriped(pix)]
    var = ma - ((mb) ** 2) + 0.05
    gap = relu(f64(rec) - mb)
    vis = var / (var + (gap) ** 2)
    lbr = relu(1.25 * vis - 0.25)
    hid = f64(unit) * (lbr - (0.8 * np.sqrt(var)))
    return unpack_fp4(w2_words, w2_scales).T @ mxq(hid, 0, "e4m3")

@@ -1,0 +1,165 @@
+import math
+from contextlib import ExitStack
+
+import concourse.mybir as mybir
+
+K, T, S, D, N, H, V, U = 512, 4096, 1024, 4, 128, 512, 256, 512
+FLOPS = 2 * K * H * S + 2 * H * N * U
+
+P = 128
+PACK = 4
+F32 = mybir.dt.float32
+BF16 = mybir.dt.bfloat16
+I32 = mybir.dt.int32
+U32 = mybir.dt.uint32
+U16 = mybir.dt.uint16
+U8 = mybir.dt.uint8
+FP8X4 = mybir.dt.float8_e4m3fn_x4
+FP4X4 = mybir.dt.float4_e2m1fn_x4
+ALU = mybir.AluOpType
+ACT = mybir.ActivationFunctionType
+HALF = 512
+RH = U // 2
+
+
+def load_scale_rows(queue, plane, rows):
+    for q in range(4):
+        queue.dma_start(out=plane[32 * q : 32 * q + 4, :].bitcast(I32), in_=rows[4 * q : 4 * q + 4, :].bitcast(I32))
+
+
+def tile_picked_ypmbps_dev_p_kernel(
+    tc, x_words, x_scales, w1_words, w1_scales, rec, unit, w2_words, w2_scales, offs, pix, out
+):
+    nc = tc.nc
+    with ExitStack() as ctx:
+        lists = ctx.enter_context(tc.tile_pool(name="lists", bufs=1))
+        keep = ctx.enter_context(tc.tile_pool(name="keep", bufs=1))
+        psum = ctx.enter_context(tc.psum_pool(name="psum", bufs=1))
+
+        offs_sb = lists.tile([P, S // 16], U16)
+        pix_sb = lists.tile([P, U // 16], U16)
+        xw = keep.tile([P, T], U32, align_bytes=64)
+        xs = keep.tile([P, T], U8, align_bytes=64)
+        w1w = keep.tile([P, 2 * H], U8, tag="w1_then_rec", align_bytes=64)
+        w1s = keep.tile([P, H], U8, align_bytes=64)
+        w2w = keep.tile([P, 2 * N], U8, align_bytes=64)
+        w2s = keep.tile([P, N], U8, align_bytes=64)
+        unit_sb = keep.tile([P, PACK], F32)
+
+        nc.vector.memset(xs[:].bitcast(I32), 0)
+        nc.gpsimd.memset(w1s[:].bitcast(I32), 0)
+        nc.gpsimd.memset(w2s[:].bitcast(I32), 0)
+        nc.sync.dma_start(offs_sb[:], offs)
+        nc.sync.dma_start(out=xw[:].bitcast(I32), in_=x_words[0].rearrange("p n b -> p (n b)").bitcast(I32))
+        nc.scalar.dma_start(out=w1w[:].bitcast(I32), in_=w1_words[0].bitcast(I32))
+        load_scale_rows(nc.scalar, xs, x_scales[0])
+        load_scale_rows(nc.gpsimd, w1s, w1_scales[0])
+        nc.sync.dma_start(pix_sb[:], pix)
+        nc.gpsimd.dma_start(out=unit_sb[:], in_=unit.rearrange("(p t) o -> p (t o)", t=PACK))
+        nc.gpsimd.dma_start(out=w2w[:].bitcast(I32), in_=w2_words[0].bitcast(I32))
+        load_scale_rows(nc.gpsimd, w2s, w2_scales[0])
+
+        w1w_dealt = keep.tile([P, 2 * H], U8, align_bytes=64)
+        w1s_dealt = keep.tile([P, H], U8, align_bytes=64)
+        nc.vector.tensor_copy(
+            out=w1w_dealt[:].rearrange("p (t m b) -> p t m b", t=PACK, b=2),
+            in_=w1w[:].rearrange("p (m t b) -> p t m b", t=PACK, b=2),
+        )
+        nc.vector.tensor_copy(
+            out=w1s_dealt[:].rearrange("p (t m) -> p t m", t=PACK),
+            in_=w1s[:].rearrange("p (m t) -> p t m", t=PACK),
+        )
+        rec_sb = keep.tile([P, PACK, U], F32, tag="w1_then_rec", align_bytes=64)
+        nc.sync.dma_start(out=rec_sb[:], in_=rec.rearrange("(p t) r -> p t r", t=PACK))
+        picked_s = keep.tile([P, S], U8, align_bytes=64)
+        nc.vector.tensor_copy(picked_s[:], xs[:].indirect(offs_sb[:]))
+        picked_w = []
+        for h in range(2):
+            pw = keep.tile([P, HALF], U32, name="picked_w%d" % h, align_bytes=64)
+            nc.vector.tensor_copy(pw[:], xw[:].indirect(offs_sb[:, h * 32 : (h + 1) * 32]))
+            picked_w.append(pw)
+
+        gain = keep.tile([P, PACK], F32)
+        nc.vector.tensor_scalar(gain[:], unit_sb[:], 0.625, None, ALU.mult)
+
+        log_win = [keep.tile([P, 8 * V], F32, name="log_win%d" % t) for t in range(PACK)]
+        dep = [w[:, 4 * V :].rearrange("p (d v) -> p d v", d=D) for w in log_win]
+        for t, h in [(0, 0), (1, 0), (0, 1), (1, 1), (2, 0), (2, 1), (3, 0), (3, 1)]:
+            y = psum.tile([P, HALF], F32, name="y", bufs=6)
+            nc.tensor.matmul_mx(
+                out=y[:],
+                lhsT=w1w_dealt[:, t * 256 : (t + 1) * 256].bitcast(FP4X4),
+                lhsT_scale=w1s_dealt[:, t * P : (t + 1) * P],
+                rhs=picked_w[h][:].bitcast(FP8X4),
+                rhs_scale=picked_s[:, h * HALF : (h + 1) * HALF],
+                start=True,
+                stop=True,
+            )
+            nc.scalar.activation(
+                out=dep[t][:, :, h * 128 : (h + 1) * 128],
+                in_=y[:].rearrange("p (v d) -> p d v", d=D),
+                func=ACT.Tanh,
+            )
+
+        mean_win = [keep.tile([P, 4 * V], F32, name="mean_win%d" % t) for t in range(PACK)]
+        squares = [keep.tile([P, 3 * V], F32, name="squares%d" % t) for t in range(PACK)]
+        log_gap = [keep.tile([P, U], F32, name="log_gap%d" % t) for t in range(PACK)]
+        arg = [keep.tile([P, U], F32, name="arg%d" % t) for t in range(PACK)]
+        shift = math.log(1.28)
+        for t in range(PACK):
+            flat = log_win[t][:, 4 * V :]
+            pair = keep.tile([P, 2 * V], F32, name="pair", bufs=2)
+            total = keep.tile([P, V], F32, name="total", bufs=2)
+            mw = mean_win[t]
+            nc.vector.tensor_tensor(pair[:], flat[:, : 2 * V], flat[:, 2 * V :], ALU.add)
+            nc.vector.tensor_tensor(mw[:, 2 * V :], flat[:, : 2 * V], flat[:, 2 * V :], ALU.subtract)
+            nc.vector.tensor_tensor(mw[:, V : 2 * V], pair[:, :V], pair[:, V:], ALU.subtract)
+            nc.vector.tensor_tensor(total[:], pair[:, :V], pair[:, V:], ALU.add)
+            nc.vector.tensor_scalar(mw[:, :V], total[:], 0.25, None, ALU.mult)
+            nc.scalar.activation(out=squares[t][:], in_=mw[:, V:], func=ACT.Square)
+        for t in range(PACK):
+            lw, sq = log_win[t], squares[t]
+            diff = keep.tile([P, U], F32, name="diff", bufs=2)
+            gap = keep.tile([P, U], F32, name="gap", bufs=2)
+            nc.vector.tensor_tensor(lw[:, 3 * V : 4 * V], sq[:, V : 2 * V], sq[:, 2 * V :], ALU.add)
+            nc.vector.tensor_tensor(diff[:], mean_win[t][:].indirect(pix_sb[:]), rec_sb[:, t, :], ALU.subtract)
+            nc.vector.scalar_tensor_tensor(lw[:, 2 * V : 3 * V], sq[:, :V], 0.5, lw[:, 3 * V : 4 * V], ALU.mult, ALU.add)
+            nc.vector.tensor_scalar(gap[:], diff[:], -1.0, 2.0**-60, ALU.mult, ALU.max)
+            nc.scalar.activation(out=lw[:, V : 2 * V], in_=lw[:, 2 * V : 3 * V], func=ACT.Ln, scale=0.125, bias=0.05)
+            nc.scalar.activation(out=log_gap[t][:], in_=gap[:], func=ACT.Ln)
+        for t in range(PACK):
+            nc.vector.tensor_scalar(log_win[t][:, :V], log_win[t][:, V : 2 * V], 0.5, shift, ALU.mult, ALU.add)
+        for t in range(PACK):
+            nc.vector.tensor_tensor(arg[t][:], log_win[t][:].indirect(pix_sb[:]), log_gap[t][:], ALU.subtract)
+        hid = keep.tile([P, PACK, U], BF16)
+        for t in range(PACK):
+            spread = keep.tile([P, U], F32, name="spread", bufs=2)
+            th = keep.tile([P, U], F32, name="th", bufs=2)
+            net = keep.tile([P, U], F32, name="net", bufs=2)
+            nc.scalar.activation(out=spread[:], in_=log_win[t][:].indirect(pix_sb[:]), func=ACT.Exp)
+            nc.scalar.activation(out=th[:], in_=arg[t][:], func=ACT.Tanh, bias=-shift)
+            nc.vector.scalar_tensor_tensor(net[:], th[:], -0.6, spread[:], ALU.max, ALU.subtract)
+            nc.vector.tensor_scalar(hid[:, t, :], net[:], 0.6, gain[:, t : t + 1], ALU.add, ALU.mult)
+
+        for g in range(2):
+            cols = slice(g * RH, (g + 1) * RH)
+            grouped = keep.tile([P, RH, PACK], BF16, name="grouped", bufs=2, align_bytes=64)
+            dst = grouped[:].rearrange("p (c i) t -> p c t i", i=4)
+            src = hid[:, :, cols].rearrange("p t (c i) -> p c t i", i=4)
+            nc.vector.tensor_copy(out=dst, in_=src)
+            codes = keep.tile([P, RH], U32, name="codes", bufs=2, align_bytes=64)
+            scales = keep.tile([P, RH], U8, name="scales", bufs=2, align_bytes=64)
+            nc.vector.quantize_mx(out=codes[:].bitcast(FP8X4), scales=scales[:], in_=grouped[:].rearrange("p r t -> p (r t)"))
+            acc = psum.tile([P, RH], F32, name="acc", bufs=2)
+            nc.tensor.matmul_mx(
+                out=acc[:],
+                lhsT=w2w[:].bitcast(FP4X4),
+                lhsT_scale=w2s[:],
+                rhs=codes[:].bitcast(FP8X4),
+                rhs_scale=scales[:],
+                start=True,
+                stop=True,
+            )
+            result = keep.tile([P, RH], F32, name="result", bufs=2)
+            nc.scalar.copy(out=result[:], in_=acc[:])
+            nc.sync.dma_start(out=out[:, cols], in_=result[:])

@@ -20,10 +20,12 @@ ALU = mybir.AluOpType
 ACT = mybir.ActivationFunctionType
 HALF = 512
 RH = U // 2
+VH = V // 2
+WIN = U + 16
 
 
-def load_scale_rows(queue, plane, rows):
-    for q in range(4):
+def load_scale_rows(queue, plane, rows, quadrants):
+    for q in quadrants:
         queue.dma_start(out=plane[32 * q : 32 * q + 4, :].bitcast(I32), in_=rows[4 * q : 4 * q + 4, :].bitcast(I32))
 
 
@@ -40,51 +42,51 @@ def tile_picked_ypmbps_dev_p_kernel(
         pix_sb = lists.tile([P, U // 16], U16)
         xw = keep.tile([P, T], U32, align_bytes=64)
         xs = keep.tile([P, T], U8, align_bytes=64)
-        w1w = keep.tile([P, 2 * H], U8, tag="w1_then_rec", align_bytes=64)
-        w1s = keep.tile([P, H], U8, align_bytes=64)
-        w2w = keep.tile([P, 2 * N], U8, align_bytes=64)
-        w2s = keep.tile([P, N], U8, align_bytes=64)
-        unit_sb = keep.tile([P, PACK], F32)
+        w1w = keep.tile([P, 2 * H], U8, tag="w1w_rec", align_bytes=64)
+        w1s = keep.tile([P, H], U8, tag="w1s_w2s", align_bytes=64)
 
         nc.vector.memset(xs[:].bitcast(I32), 0)
         nc.gpsimd.memset(w1s[:].bitcast(I32), 0)
-        nc.gpsimd.memset(w2s[:].bitcast(I32), 0)
         nc.sync.dma_start(offs_sb[:], offs)
-        nc.sync.dma_start(out=xw[:].bitcast(I32), in_=x_words[0].rearrange("p n b -> p (n b)").bitcast(I32))
         nc.scalar.dma_start(out=w1w[:].bitcast(I32), in_=w1_words[0].bitcast(I32))
-        load_scale_rows(nc.scalar, xs, x_scales[0])
-        load_scale_rows(nc.gpsimd, w1s, w1_scales[0])
+        nc.sync.dma_start(out=xw[:].bitcast(I32), in_=x_words[0].rearrange("p n b -> p (n b)").bitcast(I32))
         nc.sync.dma_start(pix_sb[:], pix)
-        nc.gpsimd.dma_start(out=unit_sb[:], in_=unit.rearrange("(p t) o -> p (t o)", t=PACK))
-        nc.gpsimd.dma_start(out=w2w[:].bitcast(I32), in_=w2_words[0].bitcast(I32))
-        load_scale_rows(nc.gpsimd, w2s, w2_scales[0])
+        load_scale_rows(nc.scalar, xs, x_scales[0], range(4))
+        load_scale_rows(nc.scalar, w1s, w1_scales[0], (0, 1))
+        load_scale_rows(nc.gpsimd, w1s, w1_scales[0], (2, 3))
 
-        w1w_dealt = keep.tile([P, 2 * H], U8, align_bytes=64)
-        w1s_dealt = keep.tile([P, H], U8, align_bytes=64)
+        mean_win = [keep.tile([P, WIN], F32, name="mean_win%d" % t) for t in range(PACK)]
+        log_win = [keep.tile([P, WIN], F32, name="log_win%d" % t) for t in range(PACK)]
+        for win in mean_win + log_win:
+            nc.gpsimd.memset(win[:, V:], 0.0)
+
+        w1w_dealt = keep.tile([P, 2 * H], U8, tag="w1w_unit", align_bytes=64)
+        w1s_dealt = keep.tile([P, H], U8, tag="w1s_w2w", align_bytes=64)
         nc.vector.tensor_copy(
             out=w1w_dealt[:].rearrange("p (t m b) -> p t m b", t=PACK, b=2),
             in_=w1w[:].rearrange("p (m t b) -> p t m b", t=PACK, b=2),
         )
+        rec_sb = keep.tile([P, PACK, U], F32, tag="w1w_rec", align_bytes=64)
+        nc.sync.dma_start(out=rec_sb[:], in_=rec.rearrange("(p t) r -> p t r", t=PACK))
+        picked_s = keep.tile([P, S], U8, align_bytes=64)
+        nc.vector.tensor_copy(picked_s[:], xs[:].indirect(offs_sb[:]))
         nc.vector.tensor_copy(
             out=w1s_dealt[:].rearrange("p (t m) -> p t m", t=PACK),
             in_=w1s[:].rearrange("p (m t) -> p t m", t=PACK),
         )
-        rec_sb = keep.tile([P, PACK, U], F32, tag="w1_then_rec", align_bytes=64)
-        nc.sync.dma_start(out=rec_sb[:], in_=rec.rearrange("(p t) r -> p t r", t=PACK))
-        picked_s = keep.tile([P, S], U8, align_bytes=64)
-        nc.vector.tensor_copy(picked_s[:], xs[:].indirect(offs_sb[:]))
         picked_w = []
         for h in range(2):
             pw = keep.tile([P, HALF], U32, name="picked_w%d" % h, align_bytes=64)
             nc.vector.tensor_copy(pw[:], xw[:].indirect(offs_sb[:, h * 32 : (h + 1) * 32]))
             picked_w.append(pw)
+        w2s = keep.tile([P, N], U8, tag="w1s_w2s", align_bytes=64)
+        nc.gpsimd.memset(w2s[:].bitcast(I32), 0)
+        load_scale_rows(nc.sync, w2s, w2_scales[0], range(4))
 
-        gain = keep.tile([P, PACK], F32)
-        nc.vector.tensor_scalar(gain[:], unit_sb[:], 0.625, None, ALU.mult)
-
-        log_win = [keep.tile([P, 8 * V], F32, name="log_win%d" % t) for t in range(PACK)]
-        dep = [w[:, 4 * V :].rearrange("p (d v) -> p d v", d=D) for w in log_win]
-        for t, h in [(0, 0), (1, 0), (0, 1), (1, 1), (2, 0), (2, 1), (3, 0), (3, 1)]:
+        dep = [keep.tile([P, 2, HALF], F32, name="dep0"), keep.tile([P, 2, HALF], F32, name="dep1"), keep.tile([P, 4, HALF], F32, name="dep2")]
+        slots = [(0, 0, dep[0][:, 0, :]), (1, 0, dep[0][:, 1, :]), (0, 1, dep[1][:, 0, :]), (1, 1, dep[1][:, 1, :])]
+        slots = slots + [(2 + j, h, dep[2][:, 2 * h + j, :]) for h in range(2) for j in range(2)]
+        for t, h, dst in slots:
             y = psum.tile([P, HALF], F32, name="y", bufs=6)
             nc.tensor.matmul_mx(
                 out=y[:],
@@ -96,53 +98,103 @@ def tile_picked_ypmbps_dev_p_kernel(
                 stop=True,
             )
             nc.scalar.activation(
-                out=dep[t][:, :, h * 128 : (h + 1) * 128],
+                out=dst.rearrange("p (d v) -> p d v", d=D),
                 in_=y[:].rearrange("p (v d) -> p d v", d=D),
                 func=ACT.Tanh,
             )
+        w2w = keep.tile([P, 2 * N], U8, tag="w1s_w2w", align_bytes=64)
+        unit_sb = keep.tile([P, PACK], F32, tag="w1w_unit", align_bytes=64)
+        nc.sync.dma_start(out=w2w[:].bitcast(I32), in_=w2_words[0].bitcast(I32))
+        nc.sync.dma_start(out=unit_sb[:], in_=unit.rearrange("(p t) o -> p (t o)", t=PACK))
 
-        mean_win = [keep.tile([P, 4 * V], F32, name="mean_win%d" % t) for t in range(PACK)]
-        squares = [keep.tile([P, 3 * V], F32, name="squares%d" % t) for t in range(PACK)]
-        log_gap = [keep.tile([P, U], F32, name="log_gap%d" % t) for t in range(PACK)]
-        arg = [keep.tile([P, U], F32, name="arg%d" % t) for t in range(PACK)]
-        shift = math.log(1.28)
-        for t in range(PACK):
-            flat = log_win[t][:, 4 * V :]
-            pair = keep.tile([P, 2 * V], F32, name="pair", bufs=2)
-            total = keep.tile([P, V], F32, name="total", bufs=2)
-            mw = mean_win[t]
-            nc.vector.tensor_tensor(pair[:], flat[:, : 2 * V], flat[:, 2 * V :], ALU.add)
-            nc.vector.tensor_tensor(mw[:, 2 * V :], flat[:, : 2 * V], flat[:, 2 * V :], ALU.subtract)
-            nc.vector.tensor_tensor(mw[:, V : 2 * V], pair[:, :V], pair[:, V:], ALU.subtract)
-            nc.vector.tensor_tensor(total[:], pair[:, :V], pair[:, V:], ALU.add)
-            nc.vector.tensor_scalar(mw[:, :V], total[:], 0.25, None, ALU.mult)
-            nc.scalar.activation(out=squares[t][:], in_=mw[:, V:], func=ACT.Square)
-        for t in range(PACK):
-            lw, sq = log_win[t], squares[t]
-            diff = keep.tile([P, U], F32, name="diff", bufs=2)
-            gap = keep.tile([P, U], F32, name="gap", bufs=2)
-            nc.vector.tensor_tensor(lw[:, 3 * V : 4 * V], sq[:, V : 2 * V], sq[:, 2 * V :], ALU.add)
-            nc.vector.tensor_tensor(diff[:], mean_win[t][:].indirect(pix_sb[:]), rec_sb[:, t, :], ALU.subtract)
-            nc.vector.scalar_tensor_tensor(lw[:, 2 * V : 3 * V], sq[:, :V], 0.5, lw[:, 3 * V : 4 * V], ALU.mult, ALU.add)
-            nc.vector.tensor_scalar(gap[:], diff[:], -1.0, 2.0**-60, ALU.mult, ALU.max)
-            nc.scalar.activation(out=lw[:, V : 2 * V], in_=lw[:, 2 * V : 3 * V], func=ACT.Ln, scale=0.125, bias=0.05)
-            nc.scalar.activation(out=log_gap[t][:], in_=gap[:], func=ACT.Ln)
-        for t in range(PACK):
-            nc.vector.tensor_scalar(log_win[t][:, :V], log_win[t][:, V : 2 * V], 0.5, shift, ALU.mult, ALU.add)
-        for t in range(PACK):
-            nc.vector.tensor_tensor(arg[t][:], log_win[t][:].indirect(pix_sb[:]), log_gap[t][:], ALU.subtract)
+        pair = [keep.tile([P, 4, 2 * VH], F32, name="pair%d" % q) for q in range(2)]
+        contrast = [keep.tile([P, 4, 3 * VH], F32, name="contrast%d" % q) for q in range(2)]
+        squares = [keep.tile([P, 4, 3 * VH], F32, name="squares%d" % q) for q in range(2)]
+        total = [keep.tile([P, 4, VH], F32, name="total%d" % q) for q in range(2)]
+        part = [keep.tile([P, 4, VH], F32, name="part%d" % q) for q in range(2)]
+        var8 = [keep.tile([P, 4, VH], F32, name="var8_%d" % q) for q in range(2)]
+        log_gap = keep.tile([P, PACK, U], F32)
+        log_var = keep.tile([P, PACK, U], F32)
+        arg = keep.tile([P, PACK, U], F32)
+        gap = keep.tile([P, PACK, U], F32)
+
+        def of_tile(planes, t):
+            return planes[t // 2][:].rearrange("p (h j) v -> p h j v", j=2)[:, :, t % 2, :]
+
+        def halves(win):
+            return win[:, :V].rearrange("p (h v) -> p h v", h=2)
+
+        def sums(src, q, rows):
+            lo, hi = src[:, :, : 2 * VH], src[:, :, 2 * VH :]
+            nc.vector.tensor_tensor(pair[q][:, rows, :], lo, hi, ALU.add)
+            nc.vector.tensor_tensor(contrast[q][:, rows, VH:], lo, hi, ALU.subtract)
+            a, b = pair[q][:, rows, :VH], pair[q][:, rows, VH:]
+            nc.vector.tensor_tensor(contrast[q][:, rows, :VH], a, b, ALU.subtract)
+            nc.vector.tensor_tensor(total[q][:, rows, :], a, b, ALU.add)
+
+        def square(q):
+            nc.scalar.activation(out=squares[q][:], in_=contrast[q][:], func=ACT.Square)
+
+        def mean(t):
+            nc.vector.tensor_scalar(halves(mean_win[t]), of_tile(total, t), -0.25, None, ALU.mult)
+
+        def partial(q):
+            nc.vector.tensor_tensor(part[q][:], squares[q][:, :, VH : 2 * VH], squares[q][:, :, 2 * VH :], ALU.add)
+
+        def variance(q):
+            nc.vector.scalar_tensor_tensor(var8[q][:], squares[q][:, :, :VH], 0.5, part[q][:], ALU.mult, ALU.add)
+
+        def log_variance(t):
+            nc.scalar.activation(out=halves(log_win[t]), in_=of_tile(var8, t), func=ACT.Ln, scale=0.125, bias=0.05)
+            nc.scalar.activation(out=log_var[:, t, :], in_=log_win[t][:].indirect(pix_sb[:]), func=ACT.Copy)
+
+        def difference(t):
+            nc.vector.tensor_tensor(arg[:, PACK - 1 - t, :], mean_win[t][:].indirect(pix_sb[:]), rec_sb[:, t, :], ALU.add)
+
+        def log_of_gap(t):
+            nc.vector.tensor_scalar(gap[:, t, :], arg[:, PACK - 1 - t, :], 2.0**-60, None, ALU.max)
+            nc.scalar.activation(out=log_gap[:, t, :], in_=gap[:, t, :], func=ACT.Ln)
+
+        sums(dep[0], 0, slice(0, 2))
+        sums(dep[1], 0, slice(2, 4))
+        square(0)
+        mean(0)
+        mean(1)
+        sums(dep[2], 1, slice(0, 4))
+        square(1)
+        partial(0)
+        mean(2)
+        variance(0)
+        mean(3)
+        log_variance(0)
+        log_variance(1)
+        difference(0)
+        partial(1)
+        log_of_gap(0)
+        variance(1)
+        log_variance(2)
+        difference(1)
+        difference(2)
+        log_of_gap(1)
+        log_variance(3)
+        difference(3)
+        log_of_gap(2)
+        log_of_gap(3)
+
+        gain = keep.tile([P, PACK], F32)
+        nc.vector.tensor_scalar(gain[:], unit_sb[:], 0.625, None, ALU.mult)
+        for ts in (slice(0, PACK - 1), slice(PACK - 1, PACK)):
+            nc.vector.scalar_tensor_tensor(arg[:, ts, :], log_var[:, ts, :], 0.5, log_gap[:, ts, :], ALU.mult, ALU.subtract)
         hid = keep.tile([P, PACK, U], BF16)
-        for t in range(PACK):
-            spread = keep.tile([P, U], F32, name="spread", bufs=2)
-            th = keep.tile([P, U], F32, name="th", bufs=2)
-            net = keep.tile([P, U], F32, name="net", bufs=2)
-            nc.scalar.activation(out=spread[:], in_=log_win[t][:].indirect(pix_sb[:]), func=ACT.Exp)
-            nc.scalar.activation(out=th[:], in_=arg[t][:], func=ACT.Tanh, bias=-shift)
-            nc.vector.scalar_tensor_tensor(net[:], th[:], -0.6, spread[:], ALU.max, ALU.subtract)
-            nc.vector.tensor_scalar(hid[:, t, :], net[:], 0.6, gain[:, t : t + 1], ALU.add, ALU.mult)
-
+        spread, th, net = log_gap, gap, log_var
         for g in range(2):
             cols = slice(g * RH, (g + 1) * RH)
+            for ts in (slice(0, 2), slice(2, 4)):
+                nc.scalar.activation(out=spread[:, ts, cols], in_=log_var[:, ts, cols], func=ACT.Exp, scale=0.5, bias=math.log(1.28))
+                nc.scalar.activation(out=th[:, ts, cols], in_=arg[:, ts, cols], func=ACT.Tanh)
+                nc.vector.scalar_tensor_tensor(net[:, ts, cols], th[:, ts, cols], -0.6, spread[:, ts, cols], ALU.max, ALU.subtract)
+            for t in range(PACK):
+                nc.vector.tensor_scalar(hid[:, t, cols], net[:, t, cols], 0.6, gain[:, t : t + 1], ALU.add, ALU.mult)
             grouped = keep.tile([P, RH, PACK], BF16, name="grouped", bufs=2, align_bytes=64)
             dst = grouped[:].rearrange("p (c i) t -> p c t i", i=4)
             src = hid[:, :, cols].rearrange("p t (c i) -> p c t i", i=4)

@@ -2,6 +2,7 @@ import math
 from contextlib import ExitStack
 
 import concourse.mybir as mybir
+from concourse.masks import make_identity
 
 K, T, S, D, N, H, V, U = 512, 4096, 1024, 4, 128, 512, 256, 512
 FLOPS = 2 * K * H * S + 2 * H * N * U
@@ -22,6 +23,7 @@ HALF = 512
 RH = U // 2
 VH = V // 2
 WIN = U + 16
+WIDE = 704
 
 
 def load_scale_rows(queue, plane, rows, quadrants):
@@ -41,111 +43,109 @@ def tile_picked_ypmbps_dev_p_kernel(
         offs_sb = lists.tile([P, S // 16], U16)
         pix_sb = lists.tile([P, U // 16], U16)
         xw = keep.tile([P, T], U32, align_bytes=64)
-        xs = keep.tile([P, T], U8, align_bytes=64)
-        w1w = keep.tile([P, 2 * H], U8, tag="w1w_rec", align_bytes=64)
-        w1s = keep.tile([P, H], U8, tag="w1s_w2s", align_bytes=64)
+        xs = keep.tile([P, T], U8, tag="xs_picked", align_bytes=64)
+        w1w = keep.tile([P, 2 * H], U8, tag="w1w_unit", align_bytes=64)
+        w1s = keep.tile([P, H], U8, tag="w1s_w2w", align_bytes=64)
+        identity = keep.tile([P, P], F32)
 
+        xs_rows = keep.tile([P, T], U8, tag="rows_rec", align_bytes=64)
+        load_scale_rows(nc.sync, xs_rows, x_scales[0], (0, 1))
+        load_scale_rows(nc.scalar, xs_rows, x_scales[0], (2, 3))
         nc.vector.memset(xs[:].bitcast(I32), 0)
         nc.gpsimd.memset(w1s[:].bitcast(I32), 0)
         nc.sync.dma_start(offs_sb[:], offs)
         nc.scalar.dma_start(out=w1w[:].bitcast(I32), in_=w1_words[0].bitcast(I32))
         nc.sync.dma_start(out=xw[:].bitcast(I32), in_=x_words[0].rearrange("p n b -> p (n b)").bitcast(I32))
         nc.sync.dma_start(pix_sb[:], pix)
-        load_scale_rows(nc.scalar, xs, x_scales[0], range(4))
+        mean_win = [keep.tile([P, WIN], F32, name="mean_win%d" % t) for t in range(PACK)]
+        log_win = [keep.tile([P, WIN if t < 3 else WIDE], F32, name="log_win%d" % t) for t in range(PACK)]
+        for t in range(PACK):
+            nc.vector.memset(mean_win[t][:, V:], 0.0)
+            nc.gpsimd.memset(log_win[t][:, V:], 0.0)
+        for q in range(4):
+            rows = slice(32 * q, 32 * q + 4)
+            nc.vector.tensor_copy(out=xs[rows, :].bitcast(I32), in_=xs_rows[rows, :].bitcast(I32))
         load_scale_rows(nc.scalar, w1s, w1_scales[0], (0, 1))
         load_scale_rows(nc.gpsimd, w1s, w1_scales[0], (2, 3))
+        make_identity(nc, identity[:])
 
-        mean_win = [keep.tile([P, WIN], F32, name="mean_win%d" % t) for t in range(PACK)]
-        log_win = [keep.tile([P, WIN], F32, name="log_win%d" % t) for t in range(PACK)]
-        for win in mean_win + log_win:
-            nc.gpsimd.memset(win[:, V:], 0.0)
-
-        w1w_dealt = keep.tile([P, 2 * H], U8, tag="w1w_unit", align_bytes=64)
-        w1s_dealt = keep.tile([P, H], U8, tag="w1s_w2w", align_bytes=64)
-        nc.vector.tensor_copy(
-            out=w1w_dealt[:].rearrange("p (t m b) -> p t m b", t=PACK, b=2),
-            in_=w1w[:].rearrange("p (m t b) -> p t m b", t=PACK, b=2),
-        )
-        rec_sb = keep.tile([P, PACK, U], F32, tag="w1w_rec", align_bytes=64)
-        nc.sync.dma_start(out=rec_sb[:], in_=rec.rearrange("(p t) r -> p t r", t=PACK))
+        listed_s = keep.tile([P, S], U8, tag="listed_w2s", align_bytes=64)
+        nc.vector.tensor_copy(listed_s[:], xs[:].indirect(offs_sb[:]))
         picked_s = keep.tile([P, S], U8, align_bytes=64)
-        nc.vector.tensor_copy(picked_s[:], xs[:].indirect(offs_sb[:]))
-        nc.vector.tensor_copy(
-            out=w1s_dealt[:].rearrange("p (t m) -> p t m", t=PACK),
-            in_=w1s[:].rearrange("p (m t) -> p t m", t=PACK),
-        )
-        picked_w = []
+        picked_w = keep.tile([P, S], U32, tag="xs_picked", align_bytes=64)
         for h in range(2):
-            pw = keep.tile([P, HALF], U32, name="picked_w%d" % h, align_bytes=64)
-            nc.vector.tensor_copy(pw[:], xw[:].indirect(offs_sb[:, h * 32 : (h + 1) * 32]))
-            picked_w.append(pw)
-        w2s = keep.tile([P, N], U8, tag="w1s_w2s", align_bytes=64)
+            cols = slice(h * HALF, (h + 1) * HALF)
+            nc.vector.tensor_copy(
+                out=picked_s[:, cols].rearrange("p (d v) -> p v d", d=D), in_=listed_s[:, cols].rearrange("p (v d) -> p v d", d=D)
+            )
+            nc.vector.tensor_copy(picked_w[:, cols].rearrange("p (d v) -> p v d", d=D), xw[:].indirect(offs_sb[:, h * 32 : (h + 1) * 32]))
+        rec_sb = keep.tile([P, PACK, U], F32, tag="rows_rec", align_bytes=64)
+        nc.sync.dma_start(out=rec_sb[:], in_=rec.rearrange("(p t) r -> p t r", t=PACK))
+
+        w2s = keep.tile([P, N], U8, tag="listed_w2s", align_bytes=64)
         nc.gpsimd.memset(w2s[:].bitcast(I32), 0)
         load_scale_rows(nc.sync, w2s, w2_scales[0], range(4))
 
-        dep = [keep.tile([P, 2, HALF], F32, name="dep0"), keep.tile([P, 2, HALF], F32, name="dep1"), keep.tile([P, 4, HALF], F32, name="dep2")]
-        slots = [(0, 0, dep[0][:, 0, :]), (1, 0, dep[0][:, 1, :]), (0, 1, dep[1][:, 0, :]), (1, 1, dep[1][:, 1, :])]
-        slots = slots + [(2 + j, h, dep[2][:, 2 * h + j, :]) for h in range(2) for j in range(2)]
-        for t, h, dst in slots:
-            y = psum.tile([P, HALF], F32, name="y", bufs=6)
+        dep = [keep.tile([P, H], F32, name="dep%d" % c) for c in range(2 * D)]
+        dep2 = [keep.tile([P, H], F32, name="dep2_%d" % c) for c in range(2 * D)]
+        for c in range(2 * D):
+            y = psum.tile([P, H], F32, name="y", tag="y_acc", bufs=4)
             nc.tensor.matmul_mx(
                 out=y[:],
-                lhsT=w1w_dealt[:, t * 256 : (t + 1) * 256].bitcast(FP4X4),
-                lhsT_scale=w1s_dealt[:, t * P : (t + 1) * P],
-                rhs=picked_w[h][:].bitcast(FP8X4),
-                rhs_scale=picked_s[:, h * HALF : (h + 1) * HALF],
+                lhsT=picked_w[:, c * P : (c + 1) * P].bitcast(FP8X4),
+                lhsT_scale=picked_s[:, c * P : (c + 1) * P],
+                rhs=w1w[:].bitcast(FP4X4),
+                rhs_scale=w1s[:],
                 start=True,
                 stop=True,
             )
             nc.scalar.activation(
-                out=dst.rearrange("p (d v) -> p d v", d=D),
-                in_=y[:].rearrange("p (v d) -> p d v", d=D),
+                out=dep[c][:].rearrange("p (t m) -> p t m", t=PACK),
+                in_=y[:].rearrange("p (m t) -> p t m", t=PACK),
                 func=ACT.Tanh,
             )
+            nc.vector.tensor_tensor(dep2[c][:], dep[c][:], dep[c][:], ALU.mult)
         w2w = keep.tile([P, 2 * N], U8, tag="w1s_w2w", align_bytes=64)
         unit_sb = keep.tile([P, PACK], F32, tag="w1w_unit", align_bytes=64)
         nc.sync.dma_start(out=w2w[:].bitcast(I32), in_=w2_words[0].bitcast(I32))
         nc.sync.dma_start(out=unit_sb[:], in_=unit.rearrange("(p t) o -> p (t o)", t=PACK))
 
-        pair = [keep.tile([P, 4, 2 * VH], F32, name="pair%d" % q) for q in range(2)]
-        contrast = [keep.tile([P, 4, 3 * VH], F32, name="contrast%d" % q) for q in range(2)]
-        squares = [keep.tile([P, 4, 3 * VH], F32, name="squares%d" % q) for q in range(2)]
-        total = [keep.tile([P, 4, VH], F32, name="total%d" % q) for q in range(2)]
-        part = [keep.tile([P, 4, VH], F32, name="part%d" % q) for q in range(2)]
-        var8 = [keep.tile([P, 4, VH], F32, name="var8_%d" % q) for q in range(2)]
+        sums = [psum.tile([P, 2 * V], F32, name="sums%d" % t) for t in range(PACK)]
+        for t, h in [(t, h) for t in range(PACK) for h in range(2)]:
+            for k, planes in enumerate((dep, dep2)):
+                for d in range(D):
+                    nc.tensor.matmul(
+                        sums[t][:, k * V + h * VH : k * V + (h + 1) * VH],
+                        planes[h * D + d][:, t * P : (t + 1) * P],
+                        identity[:],
+                        is_transpose=True,
+                        start=(d == 0),
+                        stop=(d == D - 1),
+                    )
+        mean2 = keep.tile([P, PACK, V], F32)
+        var = keep.tile([P, PACK, V], F32)
         log_gap = keep.tile([P, PACK, U], F32)
         log_var = keep.tile([P, PACK, U], F32)
         arg = keep.tile([P, PACK, U], F32)
         gap = keep.tile([P, PACK, U], F32)
 
-        def of_tile(planes, t):
-            return planes[t // 2][:].rearrange("p (h j) v -> p h j v", j=2)[:, :, t % 2, :]
-
-        def halves(win):
-            return win[:, :V].rearrange("p (h v) -> p h v", h=2)
-
-        def sums(src, q, rows):
-            lo, hi = src[:, :, : 2 * VH], src[:, :, 2 * VH :]
-            nc.vector.tensor_tensor(pair[q][:, rows, :], lo, hi, ALU.add)
-            nc.vector.tensor_tensor(contrast[q][:, rows, VH:], lo, hi, ALU.subtract)
-            a, b = pair[q][:, rows, :VH], pair[q][:, rows, VH:]
-            nc.vector.tensor_tensor(contrast[q][:, rows, :VH], a, b, ALU.subtract)
-            nc.vector.tensor_tensor(total[q][:, rows, :], a, b, ALU.add)
-
-        def square(q):
-            nc.scalar.activation(out=squares[q][:], in_=contrast[q][:], func=ACT.Square)
-
         def mean(t):
-            nc.vector.tensor_scalar(halves(mean_win[t]), of_tile(total, t), -0.25, None, ALU.mult)
+            if t != 2:
+                nc.vector.tensor_scalar(mean_win[t][:, :V], sums[t][:, :V], -0.25, None, ALU.mult)
+            else:
+                nc.scalar.activation(out=mean_win[t][:, :V], in_=sums[t][:, :V], func=ACT.Copy, scale=-0.25)
 
-        def partial(q):
-            nc.vector.tensor_tensor(part[q][:], squares[q][:, :, VH : 2 * VH], squares[q][:, :, 2 * VH :], ALU.add)
-
-        def variance(q):
-            nc.vector.scalar_tensor_tensor(var8[q][:], squares[q][:, :, :VH], 0.5, part[q][:], ALU.mult, ALU.add)
+        def mean_squared(t):
+            if t == 0:
+                nc.vector.tensor_tensor(mean2[:, t, :], mean_win[t][:, :V], mean_win[t][:, :V], ALU.mult)
+            else:
+                nc.scalar.activation(out=mean2[:, t, :], in_=sums[t][:, :V], func=ACT.Square, scale=0.25)
 
         def log_variance(t):
-            nc.scalar.activation(out=halves(log_win[t]), in_=of_tile(var8, t), func=ACT.Ln, scale=0.125, bias=0.05)
+            nc.vector.scalar_tensor_tensor(var[:, t, :], sums[t][:, V:], 0.25, mean2[:, t, :], ALU.mult, ALU.subtract)
+            nc.scalar.activation(out=log_win[t][:, :V], in_=var[:, t, :], func=ACT.Ln, bias=0.05)
+
+        def fetch_log_variance(t):
             nc.scalar.activation(out=log_var[:, t, :], in_=log_win[t][:].indirect(pix_sb[:]), func=ACT.Copy)
 
         def difference(t):
@@ -155,46 +155,53 @@ def tile_picked_ypmbps_dev_p_kernel(
             nc.vector.tensor_scalar(gap[:, t, :], arg[:, PACK - 1 - t, :], 2.0**-60, None, ALU.max)
             nc.scalar.activation(out=log_gap[:, t, :], in_=gap[:, t, :], func=ACT.Ln)
 
-        sums(dep[0], 0, slice(0, 2))
-        sums(dep[1], 0, slice(2, 4))
-        square(0)
         mean(0)
-        mean(1)
-        sums(dep[2], 1, slice(0, 4))
-        square(1)
-        partial(0)
-        mean(2)
-        variance(0)
-        mean(3)
+        mean_squared(0)
         log_variance(0)
-        log_variance(1)
+        mean_squared(1)
+        mean(1)
         difference(0)
-        partial(1)
+        fetch_log_variance(0)
+        log_variance(1)
+        mean_squared(2)
+        mean(2)
         log_of_gap(0)
-        variance(1)
-        log_variance(2)
         difference(1)
-        difference(2)
+        fetch_log_variance(1)
+        log_variance(2)
+        mean_squared(3)
+        mean(3)
         log_of_gap(1)
+        difference(2)
         log_variance(3)
+        fetch_log_variance(2)
         difference(3)
         log_of_gap(2)
         log_of_gap(3)
-
         gain = keep.tile([P, PACK], F32)
-        nc.vector.tensor_scalar(gain[:], unit_sb[:], 0.625, None, ALU.mult)
-        for ts in (slice(0, PACK - 1), slice(PACK - 1, PACK)):
-            nc.vector.scalar_tensor_tensor(arg[:, ts, :], log_var[:, ts, :], 0.5, log_gap[:, ts, :], ALU.mult, ALU.subtract)
+        nc.gpsimd.tensor_scalar(gain[:], unit_sb[:], 0.625, None, ALU.mult)
+        lift = keep.tile([P, PACK], F32)
+        nc.gpsimd.tensor_scalar(lift[:], unit_sb[:], 0.375, None, ALU.mult)
+        nc.vector.scalar_tensor_tensor(arg[:, :2, :], log_var[:, :2, :], 0.5, log_gap[:, :2, :], ALU.mult, ALU.subtract)
+        nc.vector.tensor_copy(log_var[:, 3, :], log_win[3][:].indirect(pix_sb[:]))
+        nc.vector.scalar_tensor_tensor(arg[:, 2:, :], log_var[:, 2:, :], 0.5, log_gap[:, 2:, :], ALU.mult, ALU.subtract)
         hid = keep.tile([P, PACK, U], BF16)
         spread, th, net = log_gap, gap, log_var
+
+        def visibility(ts, cols):
+            nc.scalar.activation(out=spread[:, ts, cols], in_=log_var[:, ts, cols], func=ACT.Exp, scale=0.5, bias=math.log(1.28))
+            nc.scalar.activation(out=th[:, ts, cols], in_=arg[:, ts, cols], func=ACT.Tanh)
+            nc.vector.scalar_tensor_tensor(net[:, ts, cols], th[:, ts, cols], -0.6, spread[:, ts, cols], ALU.max, ALU.subtract)
+
         for g in range(2):
             cols = slice(g * RH, (g + 1) * RH)
-            for ts in (slice(0, 2), slice(2, 4)):
-                nc.scalar.activation(out=spread[:, ts, cols], in_=log_var[:, ts, cols], func=ACT.Exp, scale=0.5, bias=math.log(1.28))
-                nc.scalar.activation(out=th[:, ts, cols], in_=arg[:, ts, cols], func=ACT.Tanh)
-                nc.vector.scalar_tensor_tensor(net[:, ts, cols], th[:, ts, cols], -0.6, spread[:, ts, cols], ALU.max, ALU.subtract)
+            visibility(slice(0, 2), cols)
+            visibility(slice(2, 4), cols)
             for t in range(PACK):
-                nc.vector.tensor_scalar(hid[:, t, cols], net[:, t, cols], 0.6, gain[:, t : t + 1], ALU.add, ALU.mult)
+                if g == 1 and t >= 2:
+                    nc.scalar.activation(out=hid[:, t, cols], in_=net[:, t, cols], func=ACT.Identity, scale=gain[:, t : t + 1], bias=lift[:, t : t + 1])
+                else:
+                    nc.vector.tensor_scalar(hid[:, t, cols], net[:, t, cols], 0.6, gain[:, t : t + 1], ALU.add, ALU.mult)
             grouped = keep.tile([P, RH, PACK], BF16, name="grouped", bufs=2, align_bytes=64)
             dst = grouped[:].rearrange("p (c i) t -> p c t i", i=4)
             src = hid[:, :, cols].rearrange("p t (c i) -> p c t i", i=4)
@@ -202,7 +209,7 @@ def tile_picked_ypmbps_dev_p_kernel(
             codes = keep.tile([P, RH], U32, name="codes", bufs=2, align_bytes=64)
             scales = keep.tile([P, RH], U8, name="scales", bufs=2, align_bytes=64)
             nc.vector.quantize_mx(out=codes[:].bitcast(FP8X4), scales=scales[:], in_=grouped[:].rearrange("p r t -> p (r t)"))
-            acc = psum.tile([P, RH], F32, name="acc", bufs=2)
+            acc = psum.tile([P, RH], F32, name="acc", tag="y_acc", bufs=4)
             nc.tensor.matmul_mx(
                 out=acc[:],
                 lhsT=w2w[:].bitcast(FP4X4),

import math
from contextlib import ExitStack

import concourse.mybir as mybir
from concourse.masks import make_identity

K, T, S, D, N, H, V, U = 512, 4096, 1024, 4, 128, 512, 256, 512
FLOPS = 2 * K * H * S + 2 * H * N * U

P = 128
PACK = 4
F32 = mybir.dt.float32
BF16 = mybir.dt.bfloat16
I32 = mybir.dt.int32
U32 = mybir.dt.uint32
U16 = mybir.dt.uint16
U8 = mybir.dt.uint8
FP8X4 = mybir.dt.float8_e4m3fn_x4
FP4X4 = mybir.dt.float4_e2m1fn_x4
ALU = mybir.AluOpType
ACT = mybir.ActivationFunctionType
HALF = 512
RH = U // 2
VH = V // 2
WIN = U + 16
WIDE = 704


def load_scale_rows(queue, plane, rows, quadrants):
    for q in quadrants:
        queue.dma_start(out=plane[32 * q : 32 * q + 4, :].bitcast(I32), in_=rows[4 * q : 4 * q + 4, :].bitcast(I32))


def tile_picked_ypmbps_dev_p_kernel(
    tc, x_words, x_scales, w1_words, w1_scales, rec, unit, w2_words, w2_scales, offs, pix, out
):
    nc = tc.nc
    with ExitStack() as ctx:
        lists = ctx.enter_context(tc.tile_pool(name="lists", bufs=1))
        keep = ctx.enter_context(tc.tile_pool(name="keep", bufs=1))
        psum = ctx.enter_context(tc.psum_pool(name="psum", bufs=1))

        offs_sb = lists.tile([P, S // 16], U16)
        pix_sb = lists.tile([P, U // 16], U16)
        xw = keep.tile([P, T], U32, align_bytes=64)
        xs = keep.tile([P, T], U8, tag="xs_picked", align_bytes=64)
        w1w = keep.tile([P, 2 * H], U8, tag="w1w_unit", align_bytes=64)
        w1s = keep.tile([P, H], U8, tag="w1s_w2w", align_bytes=64)
        identity = keep.tile([P, P], F32)

        xs_rows = keep.tile([P, T], U8, tag="rows_rec", align_bytes=64)
        load_scale_rows(nc.sync, xs_rows, x_scales[0], (0, 1))
        load_scale_rows(nc.scalar, xs_rows, x_scales[0], (2, 3))
        nc.vector.memset(xs[:].bitcast(I32), 0)
        nc.gpsimd.memset(w1s[:].bitcast(I32), 0)
        nc.sync.dma_start(offs_sb[:], offs)
        nc.scalar.dma_start(out=w1w[:].bitcast(I32), in_=w1_words[0].bitcast(I32))
        nc.sync.dma_start(out=xw[:].bitcast(I32), in_=x_words[0].rearrange("p n b -> p (n b)").bitcast(I32))
        nc.sync.dma_start(pix_sb[:], pix)
        mean_win = [keep.tile([P, WIN], F32, name="mean_win%d" % t) for t in range(PACK)]
        log_win = [keep.tile([P, WIN if t < 3 else WIDE], F32, name="log_win%d" % t) for t in range(PACK)]
        for t in range(PACK):
            nc.vector.memset(mean_win[t][:, V:], 0.0)
            nc.gpsimd.memset(log_win[t][:, V:], 0.0)
        for q in range(4):
            rows = slice(32 * q, 32 * q + 4)
            nc.vector.tensor_copy(out=xs[rows, :].bitcast(I32), in_=xs_rows[rows, :].bitcast(I32))
        load_scale_rows(nc.scalar, w1s, w1_scales[0], (0, 1))
        load_scale_rows(nc.gpsimd, w1s, w1_scales[0], (2, 3))
        make_identity(nc, identity[:])

        listed_s = keep.tile([P, S], U8, tag="listed_w2s", align_bytes=64)
        nc.vector.tensor_copy(listed_s[:], xs[:].indirect(offs_sb[:]))
        picked_s = keep.tile([P, S], U8, align_bytes=64)
        picked_w = keep.tile([P, S], U32, tag="xs_picked", align_bytes=64)
        for h in range(2):
            cols = slice(h * HALF, (h + 1) * HALF)
            nc.vector.tensor_copy(
                out=picked_s[:, cols].rearrange("p (d v) -> p v d", d=D), in_=listed_s[:, cols].rearrange("p (v d) -> p v d", d=D)
            )
            nc.vector.tensor_copy(picked_w[:, cols].rearrange("p (d v) -> p v d", d=D), xw[:].indirect(offs_sb[:, h * 32 : (h + 1) * 32]))
        rec_sb = keep.tile([P, PACK, U], F32, tag="rows_rec", align_bytes=64)
        nc.sync.dma_start(out=rec_sb[:], in_=rec.rearrange("(p t) r -> p t r", t=PACK))

        w2s = keep.tile([P, N], U8, tag="listed_w2s", align_bytes=64)
        nc.gpsimd.memset(w2s[:].bitcast(I32), 0)
        load_scale_rows(nc.sync, w2s, w2_scales[0], range(4))

        dep = [keep.tile([P, H], F32, name="dep%d" % c) for c in range(2 * D)]
        dep2 = [keep.tile([P, H], F32, name="dep2_%d" % c) for c in range(2 * D)]
        for c in range(2 * D):
            y = psum.tile([P, H], F32, name="y", tag="y_acc", bufs=4)
            nc.tensor.matmul_mx(
                out=y[:],
                lhsT=picked_w[:, c * P : (c + 1) * P].bitcast(FP8X4),
                lhsT_scale=picked_s[:, c * P : (c + 1) * P],
                rhs=w1w[:].bitcast(FP4X4),
                rhs_scale=w1s[:],
                start=True,
                stop=True,
            )
            nc.scalar.activation(
                out=dep[c][:].rearrange("p (t m) -> p t m", t=PACK),
                in_=y[:].rearrange("p (m t) -> p t m", t=PACK),
                func=ACT.Tanh,
            )
            nc.vector.tensor_tensor(dep2[c][:], dep[c][:], dep[c][:], ALU.mult)
        w2w = keep.tile([P, 2 * N], U8, tag="w1s_w2w", align_bytes=64)
        unit_sb = keep.tile([P, PACK], F32, tag="w1w_unit", align_bytes=64)
        nc.sync.dma_start(out=w2w[:].bitcast(I32), in_=w2_words[0].bitcast(I32))
        nc.sync.dma_start(out=unit_sb[:], in_=unit.rearrange("(p t) o -> p (t o)", t=PACK))

        sums = [psum.tile([P, 2 * V], F32, name="sums%d" % t) for t in range(PACK)]
        for t, h in [(t, h) for t in range(PACK) for h in range(2)]:
            for k, planes in enumerate((dep, dep2)):
                for d in range(D):
                    nc.tensor.matmul(
                        sums[t][:, k * V + h * VH : k * V + (h + 1) * VH],
                        planes[h * D + d][:, t * P : (t + 1) * P],
                        identity[:],
                        is_transpose=True,
                        start=(d == 0),
                        stop=(d == D - 1),
                    )
        mean2 = keep.tile([P, PACK, V], F32)
        var = keep.tile([P, PACK, V], F32)
        log_gap = keep.tile([P, PACK, U], F32)
        log_var = keep.tile([P, PACK, U], F32)
        arg = keep.tile([P, PACK, U], F32)
        gap = keep.tile([P, PACK, U], F32)

        def mean(t):
            if t != 2:
                nc.vector.tensor_scalar(mean_win[t][:, :V], sums[t][:, :V], -0.25, None, ALU.mult)
            else:
                nc.scalar.activation(out=mean_win[t][:, :V], in_=sums[t][:, :V], func=ACT.Copy, scale=-0.25)

        def mean_squared(t):
            if t == 0:
                nc.vector.tensor_tensor(mean2[:, t, :], mean_win[t][:, :V], mean_win[t][:, :V], ALU.mult)
            else:
                nc.scalar.activation(out=mean2[:, t, :], in_=sums[t][:, :V], func=ACT.Square, scale=0.25)

        def log_variance(t):
            nc.vector.scalar_tensor_tensor(var[:, t, :], sums[t][:, V:], 0.25, mean2[:, t, :], ALU.mult, ALU.subtract)
            nc.scalar.activation(out=log_win[t][:, :V], in_=var[:, t, :], func=ACT.Ln, bias=0.05)

        def fetch_log_variance(t):
            nc.scalar.activation(out=log_var[:, t, :], in_=log_win[t][:].indirect(pix_sb[:]), func=ACT.Copy)

        def difference(t):
            nc.vector.tensor_tensor(arg[:, PACK - 1 - t, :], mean_win[t][:].indirect(pix_sb[:]), rec_sb[:, t, :], ALU.add)

        def log_of_gap(t):
            nc.vector.tensor_scalar(gap[:, t, :], arg[:, PACK - 1 - t, :], 2.0**-60, None, ALU.max)
            nc.scalar.activation(out=log_gap[:, t, :], in_=gap[:, t, :], func=ACT.Ln)

        mean(0)
        mean_squared(0)
        log_variance(0)
        mean_squared(1)
        mean(1)
        difference(0)
        fetch_log_variance(0)
        log_variance(1)
        mean_squared(2)
        mean(2)
        log_of_gap(0)
        difference(1)
        fetch_log_variance(1)
        log_variance(2)
        mean_squared(3)
        mean(3)
        log_of_gap(1)
        difference(2)
        log_variance(3)
        fetch_log_variance(2)
        difference(3)
        log_of_gap(2)
        log_of_gap(3)
        gain = keep.tile([P, PACK], F32)
        nc.gpsimd.tensor_scalar(gain[:], unit_sb[:], 0.625, None, ALU.mult)
        lift = keep.tile([P, PACK], F32)
        nc.gpsimd.tensor_scalar(lift[:], unit_sb[:], 0.375, None, ALU.mult)
        nc.vector.scalar_tensor_tensor(arg[:, :2, :], log_var[:, :2, :], 0.5, log_gap[:, :2, :], ALU.mult, ALU.subtract)
        nc.vector.tensor_copy(log_var[:, 3, :], log_win[3][:].indirect(pix_sb[:]))
        nc.vector.scalar_tensor_tensor(arg[:, 2:, :], log_var[:, 2:, :], 0.5, log_gap[:, 2:, :], ALU.mult, ALU.subtract)
        hid = keep.tile([P, PACK, U], BF16)
        spread, th, net = log_gap, gap, log_var

        def visibility(ts, cols):
            nc.scalar.activation(out=spread[:, ts, cols], in_=log_var[:, ts, cols], func=ACT.Exp, scale=0.5, bias=math.log(1.28))
            nc.scalar.activation(out=th[:, ts, cols], in_=arg[:, ts, cols], func=ACT.Tanh)
            nc.vector.scalar_tensor_tensor(net[:, ts, cols], th[:, ts, cols], -0.6, spread[:, ts, cols], ALU.max, ALU.subtract)

        for g in range(2):
            cols = slice(g * RH, (g + 1) * RH)
            visibility(slice(0, 2), cols)
            visibility(slice(2, 4), cols)
            for t in range(PACK):
                if g == 1 and t >= 2:
                    nc.scalar.activation(out=hid[:, t, cols], in_=net[:, t, cols], func=ACT.Identity, scale=gain[:, t : t + 1], bias=lift[:, t : t + 1])
                else:
                    nc.vector.tensor_scalar(hid[:, t, cols], net[:, t, cols], 0.6, gain[:, t : t + 1], ALU.add, ALU.mult)
            grouped = keep.tile([P, RH, PACK], BF16, name="grouped", bufs=2, align_bytes=64)
            dst = grouped[:].rearrange("p (c i) t -> p c t i", i=4)
            src = hid[:, :, cols].rearrange("p t (c i) -> p c t i", i=4)
            nc.vector.tensor_copy(out=dst, in_=src)
            codes = keep.tile([P, RH], U32, name="codes", bufs=2, align_bytes=64)
            scales = keep.tile([P, RH], U8, name="scales", bufs=2, align_bytes=64)
            nc.vector.quantize_mx(out=codes[:].bitcast(FP8X4), scales=scales[:], in_=grouped[:].rearrange("p r t -> p (r t)"))
            acc = psum.tile([P, RH], F32, name="acc", tag="y_acc", bufs=4)
            nc.tensor.matmul_mx(
                out=acc[:],
                lhsT=w2w[:].bitcast(FP4X4),
                lhsT_scale=w2s[:],
                rhs=codes[:].bitcast(FP8X4),
                rhs_scale=scales[:],
                start=True,
                stop=True,
            )
            result = keep.tile([P, RH], F32, name="result", bufs=2)
            nc.scalar.copy(out=result[:], in_=acc[:])
            nc.sync.dma_start(out=out[:, cols], in_=result[:])
